import numpy as np
import ml_dtypes


def mxq(x, axis, fmt="e4m3"):
    dtype, down = {"e4m3": (ml_dtypes.float8_e4m3fn, 7), "e5m2": (ml_dtypes.float8_e5m2, 14)}[fmt]
    v = np.moveaxis(np.asarray(x, np.float32).astype(ml_dtypes.bfloat16).astype(np.float64), axis, -1)
    blocks = v.reshape(v.shape[:-1] + (-1, 32))
    amax = np.abs(blocks).max(-1, keepdims=True)
    byte = np.maximum(np.where(amax > 0, np.frexp(amax)[1] - 1 + 127, 0) - down, 1)
    scale = np.exp2(byte - 127.0)
    codes = (blocks / scale).astype(np.float32).astype(dtype).astype(np.float64)
    return np.moveaxis((codes * scale).reshape(v.shape), -1, axis)


WIDE = False


def mx_kscale(k):
    if not WIDE:
        return np.ones(k)
    levels = np.array([30, -30])
    if k % 512:
        return np.exp2(np.random.permutation(np.resize(levels, k // 32))).repeat(32)
    a = np.empty((k // 512, 16))
    for p in range(k // 512):
        a[p, :8] = np.random.permutation(np.resize(levels, 8))
        for g in range(8):
            far = levels[np.abs(levels - a[p, g]) >= 10]
            a[p, g + 8] = far[np.random.randint(len(far))]
    return np.exp2(a.ravel()).repeat(32)


def f64(x):
    return np.asarray(x).astype(np.float64)


def striped(idx):
    return np.tile(np.asarray(idx).reshape(-1, 16).T, (8, 1)).astype(np.uint16)


def unstriped(offs):
    return offs[:16].T.reshape(-1).astype(np.int64)


E2M1 = np.array([0.0, 0.5, 1.0, 1.5, 2.0, 3.0, 4.0, 6.0, -0.0, -0.5, -1.0, -1.5, -2.0, -3.0, -4.0, -6.0])


def pack_weight(w, fmt):
    k, n = w.shape
    w = f64(np.asarray(w, np.float32).astype(ml_dtypes.bfloat16)).reshape(k // 32, 32, n)
    amax = np.abs(w).max(1)
    if fmt in ("e4m3", "e5m2"):
        byte = np.frexp(amax)[1] - 1 + 127 - (7 if fmt == "e4m3" else 14)
    else:
        mant, ex = np.frexp(amax / 6.0)
        byte = np.where(mant > 0.5, ex, ex - 1) + 127
    byte = np.clip(np.where(amax > 0, byte, 1), 1, 254)
    scaled = (w * np.exp2(127.0 - byte)[:, None, :]).reshape(k, n).astype(np.float32)
    by_word = np.ascontiguousarray(scaled.reshape(k // 512, 128, 4, n).transpose(0, 1, 3, 2))
    if fmt in ("e4m3", "e5m2"):
        words = by_word.astype(ml_dtypes.float8_e4m3fn if fmt == "e4m3" else ml_dtypes.float8_e5m2).view(np.uint8)
    else:
        c = by_word.astype(ml_dtypes.float4_e2m1fn).view(np.uint8) & 0xF
        words = (c[..., 0::2] | (c[..., 1::2] << 4)).reshape(k // 512, 128, 2 * n)
    return np.ascontiguousarray(words), np.ascontiguousarray(byte.astype(np.uint8).reshape(k // 512, 16, n))


def unpack_weight(words, scales, fmt):
    g, _, n = scales.shape
    words = np.ascontiguousarray(words).reshape(g, 128, n, -1)
    if fmt in ("e4m3", "e5m2"):
        vals = words.view(ml_dtypes.float8_e4m3fn if fmt == "e4m3" else ml_dtypes.float8_e5m2).astype(np.float64)
    else:
        nib = np.empty((g, 128, n, 4), np.uint8)
        nib[..., 0::2] = words & 0xF
        nib[..., 1::2] = words >> 4
        vals = E2M1[nib]
    vals = vals * np.repeat(np.exp2(scales.astype(np.float64) - 127.0), 8, axis=1)[..., None]
    return vals.transpose(0, 1, 3, 2).reshape(g * 512, n)


def sigmoid(v):
    return 1.0 / (1.0 + np.exp(-v))


K, T, J, R, O, N, L = 512, 2048, 256, 512, 128, 256, 512


def setup_inputs():
    n = np.random.standard_normal
    idx = np.random.permutation(T)[:J]
    idx2 = np.random.permutation(T)[:J]
    idx3 = np.random.permutation(J)[:O]
    idx4 = np.random.permutation(J)[:O]
    fk = mx_kscale(K)
    fr = mx_kscale(R)
    fl = mx_kscale(L)
    xtp = pack_weight(n((K, T)) / fk[:, None], "e4m3")
    wp = pack_weight(n((K, R)) * 1 / np.sqrt(K) * fk[:, None], "e2m1")
    w2p = pack_weight(n((K, R)) * 1 / np.sqrt(K) * fk[:, None] * fr, "e5m2")
    wbp = pack_weight(n((R, N)) * 1 / np.sqrt(R) / fr[:, None], "e5m2")
    sxp = pack_weight(n((L, O)) / fl[:, None], "e2m1")
    wsp = pack_weight(n((L, N)) * 1 / np.sqrt(L) * fl[:, None], "e5m2")
    return {
        "xt_words": xtp[0],
        "xt_scales": xtp[1],
        "w_words": wp[0],
        "w_scales": wp[1],
        "w2_words": w2p[0],
        "w2_scales": w2p[1],
        "sg": (np.random.uniform(0.6, 1.6, (R, 1))).astype(np.float32),
        "bg": (np.random.uniform(-1.0, 1.0, (R, 1))).astype(np.float32),
        "wb_words": wbp[0],
        "wb_scales": wbp[1],
        "sx_words": sxp[0],
        "sx_scales": sxp[1],
        "ws_words": wsp[0],
        "ws_scales": wsp[1],
        "offs": striped(idx),
        "offs2": striped(idx2),
        "offs3": striped(idx3),
        "offs4": striped(idx4),
    }


def reference(xt_words, xt_scales, w_words, w_scales, w2_words, w2_scales, sg, bg, wb_words, wb_scales, sx_words, sx_scales, ws_words, ws_scales, offs, offs2, offs3, offs4):
    idx = unstriped(offs)
    idx2 = unstriped(offs2)
    idx3 = unstriped(offs3)
    idx4 = unstriped(offs4)
    xtu = unpack_weight(xt_words, xt_scales, "e4m3")
    wu = unpack_weight(w_words, w_scales, "e2m1")
    w2u = unpack_weight(w2_words, w2_scales, "e5m2")
    wbu = unpack_weight(wb_words, wb_scales, "e5m2")
    sxu = unpack_weight(sx_words, sx_scales, "e2m1")
    wsu = unpack_weight(ws_words, ws_scales, "e5m2")
    xtidxg = xtu[:, idx]
    a = wu.T @ xtidxg
    xtidx2g = xtu[:, idx2]
    b = w2u.T @ xtidx2g
    hid = b[:, idx4] * sigmoid(a[:, idx3] * f64(sg) + f64(bg))
    hidq = mxq(hid, 0, "e4m3")
    y = wbu.T @ hidq + wsu.T @ sxu
    return y

@@ -1,0 +1,180 @@
+from contextlib import ExitStack
+
+import concourse.mybir as mybir
+
+K, T, J, R, O, N, L = 512, 2048, 256, 512, 128, 256, 512
+FLOPS = 2 * (2 * K * R * J + R * N * O + L * N * O)
+
+F32 = mybir.dt.float32
+BF16 = mybir.dt.bfloat16
+I32 = mybir.dt.int32
+U32 = mybir.dt.uint32
+U16 = mybir.dt.uint16
+U8 = mybir.dt.uint8
+E4M3 = mybir.dt.float8_e4m3fn_x4
+E5M2 = mybir.dt.float8_e5m2_x4
+E2M1 = mybir.dt.float4_e2m1fn_x4
+ACT = mybir.ActivationFunctionType
+MULT = mybir.AluOpType.mult
+
+P = 128
+PACK = 4
+XS_SPLIT = 1408
+
+
+def load_scale_rows(queue, plane, scales, quads=range(4)):
+    for quad in quads:
+        queue.dma_start(
+            out=plane[32 * quad : 32 * quad + 4, :].bitcast(I32),
+            in_=scales[0, 4 * quad : 4 * quad + 4, :].bitcast(I32),
+        )
+
+
+def deal(copy, dealt, raw, run):
+    copy(
+        out=dealt.rearrange("p (t c i) -> p c t i", t=PACK, i=run),
+        in_=raw.rearrange("p (c i t) -> p c t i", t=PACK, i=run),
+    )
+
+
+def tile_list_ahead_gatefetch_skip_plain_kernel(
+    tc, xt_words, xt_scales, w_words, w_scales, w2_words, w2_scales, sg, bg, wb_words, wb_scales,
+    sx_words, sx_scales, ws_words, ws_scales, offs, offs2, offs3, offs4, out,
+):
+    nc = tc.nc
+    with ExitStack() as ctx:
+        sb = ctx.enter_context(tc.tile_pool(name="sb", bufs=1))
+        shared = ctx.enter_context(tc.tile_pool(name="shared", bufs=1))
+        psum = ctx.enter_context(tc.psum_pool(name="psum", bufs=1))
+
+        def tile(name, cols, dtype, tag=""):
+            return sb.tile([P, cols], dtype, name=name, tag=tag or name, align_bytes=64)
+
+        def words(ap):
+            return ap[0].rearrange("p n t -> p (n t)").bitcast(I32)
+
+        idx1 = sb.tile([P, J // 16], U16, name="idx1")
+        idx2 = sb.tile([P, J // 16], U16, name="idx2")
+        idx3 = sb.tile([P, O // 16], U16, name="idx3")
+        idx4 = sb.tile([P, O // 16], U16, name="idx4")
+        xw = tile("xw", T, U32)
+        xs = tile("xs", T, U8)
+        w_raw = tile("w_raw", R, U16)
+        w2_raw = shared.tile([P, R], U32, name="w2_raw", align_bytes=64, offset=0)
+        wsc_raw = tile("wsc_raw", R, U8)
+        w2sc_raw = shared.tile([P, R], U8, name="w2sc_raw", align_bytes=64, offset=3 * J * 4 - R // 2)
+        wb_w = tile("wb_w", N, U32)
+        ws_w = tile("ws_w", N, U32)
+        sx_w = tile("sx_w", 2 * O, U8)
+        late_sc = tile("late_sc", 2 * N + O, U8)
+        wb_s, ws_s, sx_s = late_sc[:, 0:N], late_sc[:, N : 2 * N], late_sc[:, 2 * N : 2 * N + O]
+        slope = tile("slope", PACK, F32)
+        offset = tile("offset", PACK, F32)
+
+        nc.vector.memset(xs[:, :XS_SPLIT].bitcast(I32), 0)
+        nc.gpsimd.memset(xs[:, XS_SPLIT:].bitcast(I32), 0)
+        nc.vector.memset(wsc_raw[:].bitcast(I32), 0)
+        nc.vector.memset(w2sc_raw[:].bitcast(I32), 0)
+        nc.vector.memset(late_sc[:].bitcast(I32), 0)
+
+        nc.sync.dma_start(out=idx1[:], in_=offs)
+        nc.scalar.dma_start(out=w_raw[:].bitcast(I32), in_=w_words[0].bitcast(I32))
+        nc.sync.dma_start(out=idx2[:], in_=offs2)
+        load_scale_rows(nc.scalar, xs, xt_scales, (2, 3))
+        load_scale_rows(nc.sync, xs, xt_scales, (0, 1))
+        nc.scalar.dma_start(out=xw[:].bitcast(I32), in_=words(xt_words))
+        warm_in = tile("warm_in", 1, F32)
+        warm_out = tile("warm_out", 1, F32)
+        nc.vector.memset(warm_in[:], 0.0)
+        nc.scalar.activation(out=warm_out[:], in_=warm_in[:], func=ACT.Sigmoid)
+        nc.scalar.dma_start(out=w2_raw[:].bitcast(I32), in_=words(w2_words))
+        load_scale_rows(nc.sync, wsc_raw, w_scales, (0, 1, 2))
+        load_scale_rows(nc.sync, w2sc_raw, w2_scales, (0,))
+        load_scale_rows(nc.sync, wsc_raw, w_scales, (3,))
+        load_scale_rows(nc.sync, w2sc_raw, w2_scales, (1,))
+        load_scale_rows(nc.gpsimd, w2sc_raw, w2_scales, (2, 3))
+        nc.sync.dma_start(out=idx3[:], in_=offs3)
+        nc.sync.dma_start(out=slope[:], in_=sg.rearrange("(p t) o -> p (t o)", t=PACK))
+        nc.sync.dma_start(out=offset[:], in_=bg.rearrange("(p t) o -> p (t o)", t=PACK))
+        nc.sync.dma_start(out=idx4[:], in_=offs4)
+        nc.sync.dma_start(out=ws_w[:].bitcast(I32), in_=words(ws_words))
+        nc.sync.dma_start(out=sx_w[:].bitcast(I32), in_=sx_words[0].bitcast(I32))
+        nc.sync.dma_start(out=wb_w[:].bitcast(I32), in_=words(wb_words))
+        load_scale_rows(nc.sync, ws_s, ws_scales)
+        load_scale_rows(nc.sync, sx_s, sx_scales)
+        load_scale_rows(nc.sync, wb_s, wb_scales, (0,))
+        load_scale_rows(nc.gpsimd, wb_s, wb_scales, (1, 2, 3))
+
+        w_d = tile("w_d", R, U16)
+        w2_d = tile("w2_d", R, U32)
+        wsc_d = tile("wsc_d", R, U8)
+        w2sc_d = tile("w2sc_d", R, U8)
+        deal(nc.scalar.copy, w_d[:], w_raw[:], 8)
+        deal(nc.vector.tensor_copy, wsc_d[:], wsc_raw[:], 16)
+
+        g1w = tile("g1w", J, U32)
+        g1s = tile("g1s", J, U8)
+        g2w = tile("g2w", J, U32, tag="wsc_raw")
+        g2s = tile("g2s", J, U8)
+        nc.vector.tensor_copy(out=g1s[:], in_=xs[:].indirect(idx1[:]))
+        deal(nc.scalar.copy, w2_d[:], w2_raw[:], 1)
+        nc.vector.tensor_copy(out=g2s[:], in_=xs[:].indirect(idx2[:]))
+        deal(nc.vector.tensor_copy, w2sc_d[:], w2sc_raw[:], 16)
+        nc.vector.tensor_copy(out=g1w[:], in_=xw[:].indirect(idx1[:]))
+        nc.vector.tensor_copy(out=g2w[:], in_=xw[:].indirect(idx2[:]))
+
+        gate = sb.tile([P, PACK, O], F32, name="gate", align_bytes=64)
+        picked = sb.tile([P, PACK, O], F32, name="picked", align_bytes=64)
+        for t in range(PACK):
+            cols = slice(t * P, (t + 1) * P)
+            a_ps = psum.tile([P, J], F32, name=f"a_ps{t}", tag=f"bank{t}")
+            nc.tensor.matmul_mx(
+                out=a_ps[:], lhsT=w_d[:, cols].bitcast(U8).bitcast(E2M1), lhsT_scale=wsc_d[:, cols],
+                rhs=g1w[:].bitcast(E4M3), rhs_scale=g1s[:], start=True, stop=True,
+            )
+            a_sb = shared.tile([P, J], F32, name=f"a_sb{t}", align_bytes=64, offset=t * J * 4)
+            if t < 2:
+                nc.scalar.copy(out=a_sb[:], in_=a_ps[:])
+            else:
+                nc.vector.tensor_copy(out=a_sb[:], in_=a_ps[:])
+            nc.scalar.activation(
+                out=gate[:, t, :], in_=a_sb[:].indirect(idx3[:]), func=ACT.Sigmoid,
+                bias=offset[:, t : t + 1], scale=slope[:, t : t + 1],
+            )
+            b_ps = psum.tile([P, J], F32, name=f"b_ps{t}", tag=f"bank{PACK + t}")
+            nc.tensor.matmul_mx(
+                out=b_ps[:], lhsT=w2_d[:, cols].bitcast(E5M2), lhsT_scale=w2sc_d[:, cols],
+                rhs=g2w[:].bitcast(E4M3), rhs_scale=g2s[:], start=True, stop=True,
+            )
+            b_sb = tile(f"b_sb{t}", J, F32)
+            nc.vector.tensor_copy(out=b_sb[:], in_=b_ps[:])
+            if t < 2:
+                nc.vector.tensor_copy(out=picked[:, t, :], in_=b_sb[:].indirect(idx4[:]))
+            else:
+                nc.scalar.activation(out=picked[:, t, :], in_=b_sb[:].indirect(idx4[:]), func=ACT.Copy)
+
+        hid = sb.tile([P, O, PACK], BF16, name="hid", align_bytes=64)
+        nc.vector.tensor_tensor(
+            out=hid[:], in0=picked[:].rearrange("p t o -> p o t"), in1=gate[:].rearrange("p t o -> p o t"), op=MULT,
+        )
+        hw = tile("hw", O, U32)
+        hs = tile("hs", O, U8)
+        nc.vector.quantize_mx(out=hw[:].bitcast(E4M3), scales=hs[:], in_=hid[:].rearrange("p o t -> p (o t)"))
+
+        y = sb.tile([P, 2, O], F32, name="y", align_bytes=64)
+        y_ps = [psum.tile([P, O], F32, name=f"y_ps{h}", tag=f"bank{2 * PACK - 2 + h}") for h in range(2)]
+        for h in range(2):
+            cols = slice(h * P, (h + 1) * P)
+            nc.tensor.matmul_mx(
+                out=y_ps[h][:], lhsT=ws_w[:, cols].bitcast(E5M2), lhsT_scale=ws_s[:, cols],
+                rhs=sx_w[:].bitcast(E2M1), rhs_scale=sx_s, start=True, stop=False,
+            )
+        for h in range(2):
+            cols = slice(h * P, (h + 1) * P)
+            nc.tensor.matmul_mx(
+                out=y_ps[h][:], lhsT=wb_w[:, cols].bitcast(E5M2), lhsT_scale=wb_s[:, cols],
+                rhs=hw[:].bitcast(E4M3), rhs_scale=hs[:], start=False, stop=True,
+            )
+        nc.vector.tensor_copy(out=y[:, 0, :], in_=y_ps[0][:])
+        nc.scalar.copy(out=y[:, 1, :], in_=y_ps[1][:])
+        nc.sync.dma_start(out=out.rearrange("(h p) o -> p h o", p=P), in_=y[:])

@@ -30,10 +30,10 @@ def load_scale_rows(queue, plane, scales, quads=range(4)):
         )
 
 
-def deal(copy, dealt, raw, run):
+def deal(copy, dealt, raw, run, slices=slice(0, PACK)):
     copy(
-        out=dealt.rearrange("p (t c i) -> p c t i", t=PACK, i=run),
-        in_=raw.rearrange("p (c i t) -> p c t i", t=PACK, i=run),
+        out=dealt.rearrange("p (t c i) -> p c t i", t=PACK, i=run)[:, :, slices, :],
+        in_=raw.rearrange("p (c i t) -> p c t i", t=PACK, i=run)[:, :, slices, :],
     )
 
 
@@ -73,9 +73,9 @@ def tile_list_ahead_gatefetch_skip_plain_kernel(
 
         nc.vector.memset(xs[:, :XS_SPLIT].bitcast(I32), 0)
         nc.gpsimd.memset(xs[:, XS_SPLIT:].bitcast(I32), 0)
-        nc.vector.memset(wsc_raw[:].bitcast(I32), 0)
         nc.vector.memset(w2sc_raw[:].bitcast(I32), 0)
         nc.vector.memset(late_sc[:].bitcast(I32), 0)
+        nc.vector.memset(wsc_raw[:].bitcast(I32), 0)
 
         nc.sync.dma_start(out=idx1[:], in_=offs)
         nc.scalar.dma_start(out=w_raw[:].bitcast(I32), in_=w_words[0].bitcast(I32))
@@ -97,20 +97,22 @@ def tile_list_ahead_gatefetch_skip_plain_kernel(
         nc.sync.dma_start(out=slope[:], in_=sg.rearrange("(p t) o -> p (t o)", t=PACK))
         nc.sync.dma_start(out=offset[:], in_=bg.rearrange("(p t) o -> p (t o)", t=PACK))
         nc.sync.dma_start(out=idx4[:], in_=offs4)
+        load_scale_rows(nc.sync, ws_s, ws_scales)
+        load_scale_rows(nc.sync, sx_s, sx_scales, (0,))
         nc.sync.dma_start(out=ws_w[:].bitcast(I32), in_=words(ws_words))
         nc.sync.dma_start(out=sx_w[:].bitcast(I32), in_=sx_words[0].bitcast(I32))
         nc.sync.dma_start(out=wb_w[:].bitcast(I32), in_=words(wb_words))
-        load_scale_rows(nc.sync, ws_s, ws_scales)
-        load_scale_rows(nc.sync, sx_s, sx_scales)
-        load_scale_rows(nc.sync, wb_s, wb_scales, (0,))
-        load_scale_rows(nc.gpsimd, wb_s, wb_scales, (1, 2, 3))
+        load_scale_rows(nc.sync, sx_s, sx_scales, (1, 2, 3))
+        load_scale_rows(nc.sync, wb_s, wb_scales, (0, 1))
+        load_scale_rows(nc.gpsimd, wb_s, wb_scales, (2, 3))
 
         w_d = tile("w_d", R, U16)
         w2_d = tile("w2_d", R, U32)
         wsc_d = tile("wsc_d", R, U8)
         w2sc_d = tile("w2sc_d", R, U8)
         deal(nc.scalar.copy, w_d[:], w_raw[:], 8)
-        deal(nc.vector.tensor_copy, wsc_d[:], wsc_raw[:], 16)
+        deal(nc.vector.tensor_copy, wsc_d[:], wsc_raw[:], 16, slice(0, 2))
+        deal(nc.vector.tensor_copy, wsc_d[:], wsc_raw[:], 16, slice(2, 4))
 
         g1w = tile("g1w", J, U32)
         g1s = tile("g1s", J, U8)
@@ -155,7 +157,10 @@ def tile_list_ahead_gatefetch_skip_plain_kernel(
 
         hid = sb.tile([P, O, PACK], BF16, name="hid", align_bytes=64)
         nc.vector.tensor_tensor(
-            out=hid[:], in0=picked[:].rearrange("p t o -> p o t"), in1=gate[:].rearrange("p t o -> p o t"), op=MULT,
+            out=hid[:].rearrange("p (c i) t -> p c t i", i=4),
+            in0=picked[:].rearrange("p t (c i) -> p c t i", i=4),
+            in1=gate[:].rearrange("p t (c i) -> p c t i", i=4),
+            op=MULT,
         )
         hw = tile("hw", O, U32)
         hs = tile("hs", O, U8)
@@ -177,4 +182,5 @@ def tile_list_ahead_gatefetch_skip_plain_kernel(
             )
         nc.vector.tensor_copy(out=y[:, 0, :], in_=y_ps[0][:])
         nc.scalar.copy(out=y[:, 1, :], in_=y_ps[1][:])
-        nc.sync.dma_start(out=out.rearrange("(h p) o -> p h o", p=P), in_=y[:])
+        nc.sync.dma_start(out=out[0:P, :], in_=y[:, 0, :])
+        nc.scalar.dma_start(out=out[P : 2 * P, :], in_=y[:, 1, :])

@@ -103,8 +103,8 @@ def tile_list_ahead_gatefetch_skip_plain_kernel(
         nc.sync.dma_start(out=sx_w[:].bitcast(I32), in_=sx_words[0].bitcast(I32))
         nc.sync.dma_start(out=wb_w[:].bitcast(I32), in_=words(wb_words))
         load_scale_rows(nc.sync, sx_s, sx_scales, (1, 2, 3))
-        load_scale_rows(nc.sync, wb_s, wb_scales, (0, 1))
-        load_scale_rows(nc.gpsimd, wb_s, wb_scales, (2, 3))
+        load_scale_rows(nc.sync, wb_s, wb_scales, (0,))
+        load_scale_rows(nc.gpsimd, wb_s, wb_scales, (1, 2, 3))
 
         w_d = tile("w_d", R, U16)
         w2_d = tile("w2_d", R, U32)
@@ -182,5 +182,4 @@ def tile_list_ahead_gatefetch_skip_plain_kernel(
             )
         nc.vector.tensor_copy(out=y[:, 0, :], in_=y_ps[0][:])
         nc.scalar.copy(out=y[:, 1, :], in_=y_ps[1][:])
-        nc.sync.dma_start(out=out[0:P, :], in_=y[:, 0, :])
-        nc.scalar.dma_start(out=out[P : 2 * P, :], in_=y[:, 1, :])
+        nc.sync.dma_start(out=out.rearrange("(h p) o -> p h o", p=P), in_=y[:])

from contextlib import ExitStack

import concourse.mybir as mybir

K, T, J, R, O, N, L = 512, 2048, 256, 512, 128, 256, 512
FLOPS = 2 * (2 * K * R * J + R * N * O + L * N * O)

F32 = mybir.dt.float32
BF16 = mybir.dt.bfloat16
I32 = mybir.dt.int32
U32 = mybir.dt.uint32
U16 = mybir.dt.uint16
U8 = mybir.dt.uint8
E4M3 = mybir.dt.float8_e4m3fn_x4
E5M2 = mybir.dt.float8_e5m2_x4
E2M1 = mybir.dt.float4_e2m1fn_x4
ACT = mybir.ActivationFunctionType
MULT = mybir.AluOpType.mult

P = 128
PACK = 4
XS_SPLIT = 1408


def load_scale_rows(queue, plane, scales, quads=range(4)):
    for quad in quads:
        queue.dma_start(
            out=plane[32 * quad : 32 * quad + 4, :].bitcast(I32),
            in_=scales[0, 4 * quad : 4 * quad + 4, :].bitcast(I32),
        )


def deal(copy, dealt, raw, run, slices=slice(0, PACK)):
    copy(
        out=dealt.rearrange("p (t c i) -> p c t i", t=PACK, i=run)[:, :, slices, :],
        in_=raw.rearrange("p (c i t) -> p c t i", t=PACK, i=run)[:, :, slices, :],
    )


def tile_list_ahead_gatefetch_skip_plain_kernel(
    tc, xt_words, xt_scales, w_words, w_scales, w2_words, w2_scales, sg, bg, wb_words, wb_scales,
    sx_words, sx_scales, ws_words, ws_scales, offs, offs2, offs3, offs4, out,
):
    nc = tc.nc
    with ExitStack() as ctx:
        sb = ctx.enter_context(tc.tile_pool(name="sb", bufs=1))
        shared = ctx.enter_context(tc.tile_pool(name="shared", bufs=1))
        psum = ctx.enter_context(tc.psum_pool(name="psum", bufs=1))

        def tile(name, cols, dtype, tag=""):
            return sb.tile([P, cols], dtype, name=name, tag=tag or name, align_bytes=64)

        def words(ap):
            return ap[0].rearrange("p n t -> p (n t)").bitcast(I32)

        idx1 = sb.tile([P, J // 16], U16, name="idx1")
        idx2 = sb.tile([P, J // 16], U16, name="idx2")
        idx3 = sb.tile([P, O // 16], U16, name="idx3")
        idx4 = sb.tile([P, O // 16], U16, name="idx4")
        xw = tile("xw", T, U32)
        xs = tile("xs", T, U8)
        w_raw = tile("w_raw", R, U16)
        w2_raw = shared.tile([P, R], U32, name="w2_raw", align_bytes=64, offset=0)
        wsc_raw = tile("wsc_raw", R, U8)
        w2sc_raw = shared.tile([P, R], U8, name="w2sc_raw", align_bytes=64, offset=3 * J * 4 - R // 2)
        wb_w = tile("wb_w", N, U32)
        ws_w = tile("ws_w", N, U32)
        sx_w = tile("sx_w", 2 * O, U8)
        late_sc = tile("late_sc", 2 * N + O, U8)
        wb_s, ws_s, sx_s = late_sc[:, 0:N], late_sc[:, N : 2 * N], late_sc[:, 2 * N : 2 * N + O]
        slope = tile("slope", PACK, F32)
        offset = tile("offset", PACK, F32)

        nc.vector.memset(xs[:, :XS_SPLIT].bitcast(I32), 0)
        nc.gpsimd.memset(xs[:, XS_SPLIT:].bitcast(I32), 0)
        nc.vector.memset(w2sc_raw[:].bitcast(I32), 0)
        nc.vector.memset(late_sc[:].bitcast(I32), 0)
        nc.vector.memset(wsc_raw[:].bitcast(I32), 0)

        nc.sync.dma_start(out=idx1[:], in_=offs)
        nc.scalar.dma_start(out=w_raw[:].bitcast(I32), in_=w_words[0].bitcast(I32))
        nc.sync.dma_start(out=idx2[:], in_=offs2)
        load_scale_rows(nc.scalar, xs, xt_scales, (2, 3))
        load_scale_rows(nc.sync, xs, xt_scales, (0, 1))
        nc.scalar.dma_start(out=xw[:].bitcast(I32), in_=words(xt_words))
        warm_in = tile("warm_in", 1, F32)
        warm_out = tile("warm_out", 1, F32)
        nc.vector.memset(warm_in[:], 0.0)
        nc.scalar.activation(out=warm_out[:], in_=warm_in[:], func=ACT.Sigmoid)
        nc.scalar.dma_start(out=w2_raw[:].bitcast(I32), in_=words(w2_words))
        load_scale_rows(nc.sync, wsc_raw, w_scales, (0, 1, 2))
        load_scale_rows(nc.sync, w2sc_raw, w2_scales, (0,))
        load_scale_rows(nc.sync, wsc_raw, w_scales, (3,))
        load_scale_rows(nc.sync, w2sc_raw, w2_scales, (1,))
        load_scale_rows(nc.gpsimd, w2sc_raw, w2_scales, (2, 3))
        nc.sync.dma_start(out=idx3[:], in_=offs3)
        nc.sync.dma_start(out=slope[:], in_=sg.rearrange("(p t) o -> p (t o)", t=PACK))
        nc.sync.dma_start(out=offset[:], in_=bg.rearrange("(p t) o -> p (t o)", t=PACK))
        nc.sync.dma_start(out=idx4[:], in_=offs4)
        load_scale_rows(nc.sync, ws_s, ws_scales)
        load_scale_rows(nc.sync, sx_s, sx_scales, (0,))
        nc.sync.dma_start(out=ws_w[:].bitcast(I32), in_=words(ws_words))
        nc.sync.dma_start(out=sx_w[:].bitcast(I32), in_=sx_words[0].bitcast(I32))
        nc.sync.dma_start(out=wb_w[:].bitcast(I32), in_=words(wb_words))
        load_scale_rows(nc.sync, sx_s, sx_scales, (1, 2, 3))
        load_scale_rows(nc.sync, wb_s, wb_scales, (0,))
        load_scale_rows(nc.gpsimd, wb_s, wb_scales, (1, 2, 3))

        w_d = tile("w_d", R, U16)
        w2_d = tile("w2_d", R, U32)
        wsc_d = tile("wsc_d", R, U8)
        w2sc_d = tile("w2sc_d", R, U8)
        deal(nc.scalar.copy, w_d[:], w_raw[:], 8)
        deal(nc.vector.tensor_copy, wsc_d[:], wsc_raw[:], 16, slice(0, 2))
        deal(nc.vector.tensor_copy, wsc_d[:], wsc_raw[:], 16, slice(2, 4))

        g1w = tile("g1w", J, U32)
        g1s = tile("g1s", J, U8)
        g2w = tile("g2w", J, U32, tag="wsc_raw")
        g2s = tile("g2s", J, U8)
        nc.vector.tensor_copy(out=g1s[:], in_=xs[:].indirect(idx1[:]))
        deal(nc.scalar.copy, w2_d[:], w2_raw[:], 1)
        nc.vector.tensor_copy(out=g2s[:], in_=xs[:].indirect(idx2[:]))
        deal(nc.vector.tensor_copy, w2sc_d[:], w2sc_raw[:], 16)
        nc.vector.tensor_copy(out=g1w[:], in_=xw[:].indirect(idx1[:]))
        nc.vector.tensor_copy(out=g2w[:], in_=xw[:].indirect(idx2[:]))

        gate = sb.tile([P, PACK, O], F32, name="gate", align_bytes=64)
        picked = sb.tile([P, PACK, O], F32, name="picked", align_bytes=64)
        for t in range(PACK):
            cols = slice(t * P, (t + 1) * P)
            a_ps = psum.tile([P, J], F32, name=f"a_ps{t}", tag=f"bank{t}")
            nc.tensor.matmul_mx(
                out=a_ps[:], lhsT=w_d[:, cols].bitcast(U8).bitcast(E2M1), lhsT_scale=wsc_d[:, cols],
                rhs=g1w[:].bitcast(E4M3), rhs_scale=g1s[:], start=True, stop=True,
            )
            a_sb = shared.tile([P, J], F32, name=f"a_sb{t}", align_bytes=64, offset=t * J * 4)
            if t < 2:
                nc.scalar.copy(out=a_sb[:], in_=a_ps[:])
            else:
                nc.vector.tensor_copy(out=a_sb[:], in_=a_ps[:])
            nc.scalar.activation(
                out=gate[:, t, :], in_=a_sb[:].indirect(idx3[:]), func=ACT.Sigmoid,
                bias=offset[:, t : t + 1], scale=slope[:, t : t + 1],
            )
            b_ps = psum.tile([P, J], F32, name=f"b_ps{t}", tag=f"bank{PACK + t}")
            nc.tensor.matmul_mx(
                out=b_ps[:], lhsT=w2_d[:, cols].bitcast(E5M2), lhsT_scale=w2sc_d[:, cols],
                rhs=g2w[:].bitcast(E4M3), rhs_scale=g2s[:], start=True, stop=True,
            )
            b_sb = tile(f"b_sb{t}", J, F32)
            nc.vector.tensor_copy(out=b_sb[:], in_=b_ps[:])
            if t < 2:
                nc.vector.tensor_copy(out=picked[:, t, :], in_=b_sb[:].indirect(idx4[:]))
            else:
                nc.scalar.activation(out=picked[:, t, :], in_=b_sb[:].indirect(idx4[:]), func=ACT.Copy)

        hid = sb.tile([P, O, PACK], BF16, name="hid", align_bytes=64)
        nc.vector.tensor_tensor(
            out=hid[:].rearrange("p (c i) t -> p c t i", i=4),
            in0=picked[:].rearrange("p t (c i) -> p c t i", i=4),
            in1=gate[:].rearrange("p t (c i) -> p c t i", i=4),
            op=MULT,
        )
        hw = tile("hw", O, U32)
        hs = tile("hs", O, U8)
        nc.vector.quantize_mx(out=hw[:].bitcast(E4M3), scales=hs[:], in_=hid[:].rearrange("p o t -> p (o t)"))

        y = sb.tile([P, 2, O], F32, name="y", align_bytes=64)
        y_ps = [psum.tile([P, O], F32, name=f"y_ps{h}", tag=f"bank{2 * PACK - 2 + h}") for h in range(2)]
        for h in range(2):
            cols = slice(h * P, (h + 1) * P)
            nc.tensor.matmul_mx(
                out=y_ps[h][:], lhsT=ws_w[:, cols].bitcast(E5M2), lhsT_scale=ws_s[:, cols],
                rhs=sx_w[:].bitcast(E2M1), rhs_scale=sx_s, start=True, stop=False,
            )
        for h in range(2):
            cols = slice(h * P, (h + 1) * P)
            nc.tensor.matmul_mx(
                out=y_ps[h][:], lhsT=wb_w[:, cols].bitcast(E5M2), lhsT_scale=wb_s[:, cols],
                rhs=hw[:].bitcast(E4M3), rhs_scale=hs[:], start=False, stop=True,
            )
        nc.vector.tensor_copy(out=y[:, 0, :], in_=y_ps[0][:])
        nc.scalar.copy(out=y[:, 1, :], in_=y_ps[1][:])
        nc.sync.dma_start(out=out.rearrange("(h p) o -> p h o", p=P), in_=y[:])
